import numpy as np, ml_dtypes
CORES = [2,130,10,138,18,146,26,154,34,162,42,170,50,178,58,186]
N = 16
def setup_inputs(rng):
    return {"x": rng.standard_normal((N, 128, 4096), dtype=np.float32).astype(ml_dtypes.bfloat16)}
def reference(x):
    s = np.maximum.accumulate(x, axis=0)
    y = np.full(x.shape, np.nan, x.dtype)
    y[1:] = s[:-1]
    return {"y": y}

@@ -1,0 +1,109 @@
+from concourse.bass import DstId, RemoteDMATransfer
+
+RANK_CORE = 2
+LAST = 15
+SLOTS = ((32, 6, 6), (32, 6, 7), (32, 2, 2), (32, 2, 3))
+ROW0 = tuple(sum(sl[0] for sl in SLOTS[:s]) for s in range(len(SLOTS)))
+NS = len(SLOTS)
+
+SCRATCH = {}
+for s in range(NS):
+    SCRATCH["a%d" % s] = ("dram", [16, 128, 2 * SLOTS[s][0]], "bfloat16")
+    SCRATCH["b%d" % s] = ("dram", [16, 128, 2 * SLOTS[s][0]], "bfloat16")
+SEMAPHORES = ["sent"] + [n + str(s) for s in range(NS) for n in ("ld", "fw", "ar", "rs", "st")]
+
+
+def owner_core(j, s):
+    return (j // 8) * 128 + (8 + j % 8) * 8 + SLOTS[s][2]
+
+
+def scatter(g, core, T, topo, s, rank):
+    a = T["a%d" % s]
+    h = topo.host(core)
+    for hh in (h, 1 - h):
+        trs = []
+        for e in range(8):
+            j = hh * 8 + e
+            rid, pid = topo.addr(owner_core(j, s), core)
+            trs.append(RemoteDMATransfer(dst_ids=[DstId(rid=rid, pnc=pid)], dma_engine_mask=1 << e,
+                                         remote_sem=T.sem["ar%d" % s], src=a[j], dst=a[rank]))
+        g.remote_dma_fused(trs, local_sem=T.sem.sent)
+    return 16
+
+
+def run_rank(g, core, T, topo, rank):
+    q = (g.sync, g.scalar)
+    sent = 0
+    if rank < LAST:
+        for s in range(NS):
+            n = SLOTS[s][0]
+            q[s % 2].dma_start(T["a%d" % s][:], T.x[ROW0[s]:ROW0[s] + n, :]).then_inc(T.sem["ld%d" % s], 16)
+        for s in range(NS):
+            g.wait_ge(T.sem["ld%d" % s], 16)
+            if SLOTS[s][1] == RANK_CORE:
+                sent += scatter(g, core, T, topo, s, rank)
+            else:
+                a = T["a%d" % s]
+                rid, pid = topo.addr(core - RANK_CORE + SLOTS[s][1], core)
+                g.remote_dma_fused(
+                    [RemoteDMATransfer(dst_ids=[DstId(rid=rid, pnc=pid)], dma_engine_mask=1 << j,
+                                       remote_sem=T.sem["fw%d" % s], src=a[j], dst=a[j]) for j in range(16)],
+                    local_sem=T.sem.sent)
+                sent += 16
+    if rank > 0:
+        for s in range(NS):
+            qq = q[0] if SLOTS[s][1] == RANK_CORE else q[1]
+            n = SLOTS[s][0]
+            qq.wait_ge(T.sem["rs%d" % s], 16)
+            qq.dma_start(T.y[ROW0[s]:ROW0[s] + n, :], T["b%d" % s][:]).then_inc(T.sem["st%d" % s], 16)
+    if sent:
+        g.wait_ge(T.sem.sent, sent)
+    if rank > 0:
+        for s in range(NS):
+            g.wait_ge(T.sem["st%d" % s], 16)
+
+
+def run_helper(g, core, T, topo, rank):
+    sent = 0
+    for s in range(NS):
+        if SLOTS[s][1] == core % 8:
+            g.wait_ge(T.sem["fw%d" % s], 16)
+            sent += scatter(g, core, T, topo, s, rank)
+    if sent:
+        g.wait_ge(T.sem.sent, sent)
+
+
+def run_owner(g, core, T, topo):
+    j = topo.host(core) * 8 + topo.chip(core) - 8
+    sent = 0
+    for s in range(NS):
+        if SLOTS[s][2] != core % 8:
+            continue
+        a, b = T["a%d" % s], T["b%d" % s]
+        g.wait_ge(T.sem["ar%d" % s], LAST)
+        for ranks in (range(15, 7, -1), range(1, 8)):
+            trs = []
+            for e, r in enumerate(ranks):
+                rid, pid = topo.addr(T.cores[r], core)
+                d = [DstId(rid=rid, pnc=pid)]
+                if r == 1:
+                    trs.append(RemoteDMATransfer(dst_ids=d, dma_engine_mask=1 << e, remote_sem=T.sem["rs%d" % s],
+                                                 src=a[0], dst=b[j]))
+                else:
+                    trs.append(RemoteDMATransfer(dst_ids=d, dma_engine_mask=1 << e, remote_sem=T.sem["rs%d" % s],
+                                                 srcs=[a[k] for k in range(r)], dsts=[b[j]], alu_op=2))
+            g.remote_dma_fused(trs, local_sem=T.sem.sent)
+            sent += len(trs)
+    if sent:
+        g.wait_ge(T.sem.sent, sent)
+
+
+def rank_program(g, core, T, topo):
+    if topo.chip(core) >= 8:
+        run_owner(g, core, T, topo)
+        return
+    rank = T.rank_of(core - core % 8 + RANK_CORE)
+    if core % 8 == RANK_CORE:
+        run_rank(g, core, T, topo, rank)
+    elif rank < LAST:
+        run_helper(g, core, T, topo, rank)

@@ -2,7 +2,8 @@ from concourse.bass import DstId, RemoteDMATransfer
 
 RANK_CORE = 2
 LAST = 15
-SLOTS = ((32, 6, 6), (32, 6, 7), (32, 2, 2), (32, 2, 3))
+HALF = 8
+SLOTS = ((32, 6, 6, 2), (32, 6, 7, 3), (32, 2, 2, 6), (32, 2, 3, 7))
 ROW0 = tuple(sum(sl[0] for sl in SLOTS[:s]) for s in range(len(SLOTS)))
 NS = len(SLOTS)
 
@@ -13,8 +14,8 @@ for s in range(NS):
 SEMAPHORES = ["sent"] + [n + str(s) for s in range(NS) for n in ("ld", "fw", "ar", "rs", "st")]
 
 
-def owner_core(j, s):
-    return (j // 8) * 128 + (8 + j % 8) * 8 + SLOTS[s][2]
+def fold_core(j, s, rank):
+    return (j // 8) * 128 + (8 + j % 8) * 8 + SLOTS[s][2 if rank < HALF else 3]
 
 
 def scatter(g, core, T, topo, s, rank):
@@ -24,7 +25,7 @@ def scatter(g, core, T, topo, s, rank):
         trs = []
         for e in range(8):
             j = hh * 8 + e
-            rid, pid = topo.addr(owner_core(j, s), core)
+            rid, pid = topo.addr(fold_core(j, s, rank), core)
             trs.append(RemoteDMATransfer(dst_ids=[DstId(rid=rid, pnc=pid)], dma_engine_mask=1 << e,
                                          remote_sem=T.sem["ar%d" % s], src=a[j], dst=a[rank]))
         g.remote_dma_fused(trs, local_sem=T.sem.sent)
@@ -54,7 +55,7 @@ def run_rank(g, core, T, topo, rank):
         for s in range(NS):
             qq = q[0] if SLOTS[s][1] == RANK_CORE else q[1]
             n = SLOTS[s][0]
-            qq.wait_ge(T.sem["rs%d" % s], 16)
+            qq.wait_ge(T.sem["rs%d" % s], 32)
             qq.dma_start(T.y[ROW0[s]:ROW0[s] + n, :], T["b%d" % s][:]).then_inc(T.sem["st%d" % s], 16)
     if sent:
         g.wait_ge(T.sem.sent, sent)
@@ -73,34 +74,46 @@ def run_helper(g, core, T, topo, rank):
         g.wait_ge(T.sem.sent, sent)
 
 
-def run_owner(g, core, T, topo):
+def folds(g, core, T, topo, s, j, ranks, extra):
+    a, b = T["a%d" % s], T["b%d" % s]
+    trs = list(extra)
+    for i, r in enumerate(ranks):
+        rid, pid = topo.addr(T.cores[r], core)
+        srcs = [a[k] for k in range(r)] if r <= HALF else [a[LAST]] + [a[k] for k in range(HALF, r)]
+        if len(srcs) == 1:
+            trs.append(RemoteDMATransfer(dst_ids=[DstId(rid=rid, pnc=pid)], dma_engine_mask=3 << (2 * i),
+                                         remote_sem=T.sem["rs%d" % s], src=srcs[0], dst=b[j]))
+        else:
+            trs.append(RemoteDMATransfer(dst_ids=[DstId(rid=rid, pnc=pid)], dma_engine_mask=3 << (2 * i),
+                                         remote_sem=T.sem["rs%d" % s], srcs=srcs, dsts=[b[j]], alu_op=2))
+    g.remote_dma_fused(trs, local_sem=T.sem.sent)
+    return 2 * len(ranks) + 8 * len(extra)
+
+
+def run_folder(g, core, T, topo):
     j = topo.host(core) * 8 + topo.chip(core) - 8
+    low = [s for s in range(NS) if SLOTS[s][2] == core % 8]
+    high = [s for s in range(NS) if SLOTS[s][3] == core % 8]
     sent = 0
-    for s in range(NS):
-        if SLOTS[s][2] != core % 8:
-            continue
-        a, b = T["a%d" % s], T["b%d" % s]
-        g.wait_ge(T.sem["ar%d" % s], LAST)
-        for ranks in (range(15, 7, -1), range(1, 8)):
-            trs = []
-            for e, r in enumerate(ranks):
-                rid, pid = topo.addr(T.cores[r], core)
-                d = [DstId(rid=rid, pnc=pid)]
-                if r == 1:
-                    trs.append(RemoteDMATransfer(dst_ids=d, dma_engine_mask=1 << e, remote_sem=T.sem["rs%d" % s],
-                                                 src=a[0], dst=b[j]))
-                else:
-                    trs.append(RemoteDMATransfer(dst_ids=d, dma_engine_mask=1 << e, remote_sem=T.sem["rs%d" % s],
-                                                 srcs=[a[k] for k in range(r)], dsts=[b[j]], alu_op=2))
-            g.remote_dma_fused(trs, local_sem=T.sem.sent)
-            sent += len(trs)
+    for s in low:
+        a = T["a%d" % s]
+        g.wait_ge(T.sem["ar%d" % s], HALF)
+        rid, pid = topo.addr(core - core % 8 + SLOTS[s][3], core)
+        m8 = RemoteDMATransfer(dst_ids=[DstId(rid=rid, pnc=pid)], dma_engine_mask=0xFF00, remote_sem=T.sem["ar%d" % s],
+                               srcs=[a[k] for k in range(HALF)], dsts=[a[LAST]], alu_op=2)
+        sent += folds(g, core, T, topo, s, j, (8, 7, 6, 5), [m8])
+        sent += folds(g, core, T, topo, s, j, (1, 2, 3, 4), [])
+    for s in high:
+        g.wait_ge(T.sem["ar%d" % s], LAST - HALF + 8)
+        sent += folds(g, core, T, topo, s, j, (15, 14, 13, 12), [])
+        sent += folds(g, core, T, topo, s, j, (9, 10, 11), [])
     if sent:
         g.wait_ge(T.sem.sent, sent)
 
 
 def rank_program(g, core, T, topo):
     if topo.chip(core) >= 8:
-        run_owner(g, core, T, topo)
+        run_folder(g, core, T, topo)
         return
     rank = T.rank_of(core - core % 8 + RANK_CORE)
     if core % 8 == RANK_CORE:

@@ -6,12 +6,14 @@ HALF = 8
 SLOTS = ((32, 6, 6, 2), (32, 6, 7, 3), (32, 2, 2, 6), (32, 2, 3, 7))
 ROW0 = tuple(sum(sl[0] for sl in SLOTS[:s]) for s in range(len(SLOTS)))
 NS = len(SLOTS)
+LOW_RANKS = ((8, 5, 4, 1), (7, 6, 3, 2))
+HIGH_RANKS = ((9, 12, 13), (10, 11, 14, 15))
 
 SCRATCH = {}
 for s in range(NS):
     SCRATCH["a%d" % s] = ("dram", [16, 128, 2 * SLOTS[s][0]], "bfloat16")
     SCRATCH["b%d" % s] = ("dram", [16, 128, 2 * SLOTS[s][0]], "bfloat16")
-SEMAPHORES = ["sent"] + [n + str(s) for s in range(NS) for n in ("ld", "fw", "ar", "rs", "st")]
+SEMAPHORES = ["sent"] + [n + str(s) for s in range(NS) for n in ("ld", "fw", "ar", "ah", "m8", "rs", "st")]
 
 
 def fold_core(j, s, rank):
@@ -20,6 +22,7 @@ def fold_core(j, s, rank):
 
 def scatter(g, core, T, topo, s, rank):
     a = T["a%d" % s]
+    sem = T.sem[("ar%d" if rank < HALF else "ah%d") % s]
     h = topo.host(core)
     for hh in (h, 1 - h):
         trs = []
@@ -27,7 +30,7 @@ def scatter(g, core, T, topo, s, rank):
             j = hh * 8 + e
             rid, pid = topo.addr(fold_core(j, s, rank), core)
             trs.append(RemoteDMATransfer(dst_ids=[DstId(rid=rid, pnc=pid)], dma_engine_mask=1 << e,
-                                         remote_sem=T.sem["ar%d" % s], src=a[j], dst=a[rank]))
+                                         remote_sem=sem, src=a[j], dst=a[rank]))
         g.remote_dma_fused(trs, local_sem=T.sem.sent)
     return 16
 
@@ -74,6 +77,13 @@ def run_helper(g, core, T, topo, rank):
         g.wait_ge(T.sem.sent, sent)
 
 
+def copies(core, T, topo, s, ks, sem):
+    a = T["a%d" % s]
+    rid, pid = topo.addr(core - 2, core)
+    return [RemoteDMATransfer(dst_ids=[DstId(rid=rid, pnc=pid)], dma_engine_mask=1 << (8 + i), remote_sem=sem,
+                              src=a[k], dst=a[k]) for i, k in enumerate(ks)]
+
+
 def folds(g, core, T, topo, s, j, ranks, extra):
     a, b = T["a%d" % s], T["b%d" % s]
     trs = list(extra)
@@ -87,28 +97,39 @@ def folds(g, core, T, topo, s, j, ranks, extra):
             trs.append(RemoteDMATransfer(dst_ids=[DstId(rid=rid, pnc=pid)], dma_engine_mask=3 << (2 * i),
                                          remote_sem=T.sem["rs%d" % s], srcs=srcs, dsts=[b[j]], alu_op=2))
     g.remote_dma_fused(trs, local_sem=T.sem.sent)
-    return 2 * len(ranks) + 8 * len(extra)
+    return 2 * len(ranks) + len(extra)
 
 
 def run_folder(g, core, T, topo):
     j = topo.host(core) * 8 + topo.chip(core) - 8
-    low = [s for s in range(NS) if SLOTS[s][2] == core % 8]
-    high = [s for s in range(NS) if SLOTS[s][3] == core % 8]
+    par = topo.chip(core) % 2
+    port = core % 8 in (2, 3, 6, 7)
+    lead = core % 8 if port else core % 8 + 2
+    plane = 1 - par if port else par
+    lo = [s for s in range(NS) if SLOTS[s][2] == lead][0]
+    hi = [s for s in range(NS) if SLOTS[s][3] == lead][0]
     sent = 0
-    for s in low:
-        a = T["a%d" % s]
-        g.wait_ge(T.sem["ar%d" % s], HALF)
-        rid, pid = topo.addr(core - core % 8 + SLOTS[s][3], core)
-        m8 = RemoteDMATransfer(dst_ids=[DstId(rid=rid, pnc=pid)], dma_engine_mask=0xFF00, remote_sem=T.sem["ar%d" % s],
-                               srcs=[a[k] for k in range(HALF)], dsts=[a[LAST]], alu_op=2)
-        sent += folds(g, core, T, topo, s, j, (8, 7, 6, 5), [m8])
-        sent += folds(g, core, T, topo, s, j, (1, 2, 3, 4), [])
-    for s in high:
-        g.wait_ge(T.sem["ar%d" % s], LAST - HALF + 8)
-        sent += folds(g, core, T, topo, s, j, (15, 14, 13, 12), [])
-        sent += folds(g, core, T, topo, s, j, (9, 10, 11), [])
-    if sent:
-        g.wait_ge(T.sem.sent, sent)
+    g.wait_ge(T.sem["ar%d" % lo], HALF)
+    extra = copies(core, T, topo, lo, range(HALF), T.sem["ar%d" % lo]) if port else []
+    sent += folds(g, core, T, topo, lo, j, LOW_RANKS[plane], extra)
+    if port:
+        a = T["a%d" % lo]
+        base = core - core % 8
+        ids = []
+        for d in (base + SLOTS[lo][3], base + SLOTS[lo][3] - 2):
+            rid, pid = topo.addr(d, core)
+            ids.append(DstId(rid=rid, pnc=pid))
+        g.remote_dma_fused([RemoteDMATransfer(dst_ids=ids, dma_engine_mask=0xFF00, remote_sem=T.sem["m8%d" % lo],
+                                              srcs=[a[k] for k in range(HALF)], dsts=[a[LAST], a[LAST]], alu_op=2)],
+                           local_sem=T.sem.sent)
+        sent += 8
+    g.wait_ge(T.sem["ah%d" % hi], LAST - HALF)
+    if port:
+        g.remote_dma_fused(copies(core, T, topo, hi, range(HALF, LAST), T.sem["ah%d" % hi]), local_sem=T.sem.sent)
+        sent += LAST - HALF
+    g.wait_ge(T.sem["m8%d" % hi], 8)
+    sent += folds(g, core, T, topo, hi, j, HIGH_RANKS[plane], [])
+    g.wait_ge(T.sem.sent, sent)
 
 
 def rank_program(g, core, T, topo):

@@ -17,7 +17,7 @@ SEMAPHORES = ["sent"] + [n + str(s) for s in range(NS) for n in ("ld", "fw", "ar
 
 
 def fold_core(j, s, rank):
-    return (j // 8) * 128 + (8 + j % 8) * 8 + SLOTS[s][2 if rank < HALF else 3]
+    return (j // 8) * 128 + (8 + j % 8) * 8 + (SLOTS[s][2] if rank < HALF else SLOTS[s][3] - 2)
 
 
 def scatter(g, core, T, topo, s, rank):
@@ -77,9 +77,9 @@ def run_helper(g, core, T, topo, rank):
         g.wait_ge(T.sem.sent, sent)
 
 
-def copies(core, T, topo, s, ks, sem):
+def copies(core, T, topo, s, ks, sem, to):
     a = T["a%d" % s]
-    rid, pid = topo.addr(core - 2, core)
+    rid, pid = topo.addr(to, core)
     return [RemoteDMATransfer(dst_ids=[DstId(rid=rid, pnc=pid)], dma_engine_mask=1 << (8 + i), remote_sem=sem,
                               src=a[k], dst=a[k]) for i, k in enumerate(ks)]
 
@@ -109,8 +109,13 @@ def run_folder(g, core, T, topo):
     lo = [s for s in range(NS) if SLOTS[s][2] == lead][0]
     hi = [s for s in range(NS) if SLOTS[s][3] == lead][0]
     sent = 0
+    if not port:
+        g.wait_ge(T.sem["ah%d" % hi], LAST - HALF)
+        g.remote_dma_fused(copies(core, T, topo, hi, range(HALF, LAST), T.sem["ah%d" % hi], core + 2),
+                           local_sem=T.sem.sent)
+        sent += LAST - HALF
     g.wait_ge(T.sem["ar%d" % lo], HALF)
-    extra = copies(core, T, topo, lo, range(HALF), T.sem["ar%d" % lo]) if port else []
+    extra = copies(core, T, topo, lo, range(HALF), T.sem["ar%d" % lo], core - 2) if port else []
     sent += folds(g, core, T, topo, lo, j, LOW_RANKS[plane], extra)
     if port:
         a = T["a%d" % lo]
@@ -123,10 +128,7 @@ def run_folder(g, core, T, topo):
                                               srcs=[a[k] for k in range(HALF)], dsts=[a[LAST], a[LAST]], alu_op=2)],
                            local_sem=T.sem.sent)
         sent += 8
-    g.wait_ge(T.sem["ah%d" % hi], LAST - HALF)
-    if port:
-        g.remote_dma_fused(copies(core, T, topo, hi, range(HALF, LAST), T.sem["ah%d" % hi]), local_sem=T.sem.sent)
-        sent += LAST - HALF
+        g.wait_ge(T.sem["ah%d" % hi], LAST - HALF)
     g.wait_ge(T.sem["m8%d" % hi], 8)
     sent += folds(g, core, T, topo, hi, j, HIGH_RANKS[plane], [])
     g.wait_ge(T.sem.sent, sent)

from concourse.bass import DstId, RemoteDMATransfer

RANK_CORE = 2
LAST = 15
HALF = 8
SLOTS = ((32, 6, 6, 2), (32, 6, 7, 3), (32, 2, 2, 6), (32, 2, 3, 7))
ROW0 = tuple(sum(sl[0] for sl in SLOTS[:s]) for s in range(len(SLOTS)))
NS = len(SLOTS)
LOW_RANKS = ((8, 5, 4, 1), (7, 6, 3, 2))
HIGH_RANKS = ((9, 12, 13), (10, 11, 14, 15))

SCRATCH = {}
for s in range(NS):
    SCRATCH["a%d" % s] = ("dram", [16, 128, 2 * SLOTS[s][0]], "bfloat16")
    SCRATCH["b%d" % s] = ("dram", [16, 128, 2 * SLOTS[s][0]], "bfloat16")
SEMAPHORES = ["sent"] + [n + str(s) for s in range(NS) for n in ("ld", "fw", "ar", "ah", "m8", "rs", "st")]


def fold_core(j, s, rank):
    return (j // 8) * 128 + (8 + j % 8) * 8 + (SLOTS[s][2] if rank < HALF else SLOTS[s][3] - 2)


def scatter(g, core, T, topo, s, rank):
    a = T["a%d" % s]
    sem = T.sem[("ar%d" if rank < HALF else "ah%d") % s]
    h = topo.host(core)
    for hh in (h, 1 - h):
        trs = []
        for e in range(8):
            j = hh * 8 + e
            rid, pid = topo.addr(fold_core(j, s, rank), core)
            trs.append(RemoteDMATransfer(dst_ids=[DstId(rid=rid, pnc=pid)], dma_engine_mask=1 << e,
                                         remote_sem=sem, src=a[j], dst=a[rank]))
        g.remote_dma_fused(trs, local_sem=T.sem.sent)
    return 16


def run_rank(g, core, T, topo, rank):
    q = (g.sync, g.scalar)
    sent = 0
    if rank < LAST:
        for s in range(NS):
            n = SLOTS[s][0]
            q[s % 2].dma_start(T["a%d" % s][:], T.x[ROW0[s]:ROW0[s] + n, :]).then_inc(T.sem["ld%d" % s], 16)
        for s in range(NS):
            g.wait_ge(T.sem["ld%d" % s], 16)
            if SLOTS[s][1] == RANK_CORE:
                sent += scatter(g, core, T, topo, s, rank)
            else:
                a = T["a%d" % s]
                rid, pid = topo.addr(core - RANK_CORE + SLOTS[s][1], core)
                g.remote_dma_fused(
                    [RemoteDMATransfer(dst_ids=[DstId(rid=rid, pnc=pid)], dma_engine_mask=1 << j,
                                       remote_sem=T.sem["fw%d" % s], src=a[j], dst=a[j]) for j in range(16)],
                    local_sem=T.sem.sent)
                sent += 16
    if rank > 0:
        for s in range(NS):
            qq = q[0] if SLOTS[s][1] == RANK_CORE else q[1]
            n = SLOTS[s][0]
            qq.wait_ge(T.sem["rs%d" % s], 32)
            qq.dma_start(T.y[ROW0[s]:ROW0[s] + n, :], T["b%d" % s][:]).then_inc(T.sem["st%d" % s], 16)
    if sent:
        g.wait_ge(T.sem.sent, sent)
    if rank > 0:
        for s in range(NS):
            g.wait_ge(T.sem["st%d" % s], 16)


def run_helper(g, core, T, topo, rank):
    sent = 0
    for s in range(NS):
        if SLOTS[s][1] == core % 8:
            g.wait_ge(T.sem["fw%d" % s], 16)
            sent += scatter(g, core, T, topo, s, rank)
    if sent:
        g.wait_ge(T.sem.sent, sent)


def copies(core, T, topo, s, ks, sem, to):
    a = T["a%d" % s]
    rid, pid = topo.addr(to, core)
    return [RemoteDMATransfer(dst_ids=[DstId(rid=rid, pnc=pid)], dma_engine_mask=1 << (8 + i), remote_sem=sem,
                              src=a[k], dst=a[k]) for i, k in enumerate(ks)]


def folds(g, core, T, topo, s, j, ranks, extra):
    a, b = T["a%d" % s], T["b%d" % s]
    trs = list(extra)
    for i, r in enumerate(ranks):
        rid, pid = topo.addr(T.cores[r], core)
        srcs = [a[k] for k in range(r)] if r <= HALF else [a[LAST]] + [a[k] for k in range(HALF, r)]
        if len(srcs) == 1:
            trs.append(RemoteDMATransfer(dst_ids=[DstId(rid=rid, pnc=pid)], dma_engine_mask=3 << (2 * i),
                                         remote_sem=T.sem["rs%d" % s], src=srcs[0], dst=b[j]))
        else:
            trs.append(RemoteDMATransfer(dst_ids=[DstId(rid=rid, pnc=pid)], dma_engine_mask=3 << (2 * i),
                                         remote_sem=T.sem["rs%d" % s], srcs=srcs, dsts=[b[j]], alu_op=2))
    g.remote_dma_fused(trs, local_sem=T.sem.sent)
    return 2 * len(ranks) + len(extra)


def run_folder(g, core, T, topo):
    j = topo.host(core) * 8 + topo.chip(core) - 8
    par = topo.chip(core) % 2
    port = core % 8 in (2, 3, 6, 7)
    lead = core % 8 if port else core % 8 + 2
    plane = 1 - par if port else par
    lo = [s for s in range(NS) if SLOTS[s][2] == lead][0]
    hi = [s for s in range(NS) if SLOTS[s][3] == lead][0]
    sent = 0
    if not port:
        g.wait_ge(T.sem["ah%d" % hi], LAST - HALF)
        g.remote_dma_fused(copies(core, T, topo, hi, range(HALF, LAST), T.sem["ah%d" % hi], core + 2),
                           local_sem=T.sem.sent)
        sent += LAST - HALF
    g.wait_ge(T.sem["ar%d" % lo], HALF)
    extra = copies(core, T, topo, lo, range(HALF), T.sem["ar%d" % lo], core - 2) if port else []
    sent += folds(g, core, T, topo, lo, j, LOW_RANKS[plane], extra)
    if port:
        a = T["a%d" % lo]
        base = core - core % 8
        ids = []
        for d in (base + SLOTS[lo][3], base + SLOTS[lo][3] - 2):
            rid, pid = topo.addr(d, core)
            ids.append(DstId(rid=rid, pnc=pid))
        g.remote_dma_fused([RemoteDMATransfer(dst_ids=ids, dma_engine_mask=0xFF00, remote_sem=T.sem["m8%d" % lo],
                                              srcs=[a[k] for k in range(HALF)], dsts=[a[LAST], a[LAST]], alu_op=2)],
                           local_sem=T.sem.sent)
        sent += 8
        g.wait_ge(T.sem["ah%d" % hi], LAST - HALF)
    g.wait_ge(T.sem["m8%d" % hi], 8)
    sent += folds(g, core, T, topo, hi, j, HIGH_RANKS[plane], [])
    g.wait_ge(T.sem.sent, sent)


def rank_program(g, core, T, topo):
    if topo.chip(core) >= 8:
        run_folder(g, core, T, topo)
        return
    rank = T.rank_of(core - core % 8 + RANK_CORE)
    if core % 8 == RANK_CORE:
        run_rank(g, core, T, topo, rank)
    elif rank < LAST:
        run_helper(g, core, T, topo, rank)
